import numpy as np, ml_dtypes
CORES = [16,32,48,64,80]
N = 5
import mx_ref
NC, G, D = 256, 2, 4
C = np.float32(0.031)
BF = ml_dtypes.bfloat16
def cut(t, i, w=512):
    return t[:, w * i:w * i + w]
def tile(rs):
    return np.stack(rs, axis=2).reshape(128, -1).astype(BF)
def act(Z):
    return [np.maximum(s * z, 0) * C for z in Z for s in (1, -1)]
def taps(w, i, e):
    return mx_ref.matmul(mx_ref.quantize(cut(w, 2 * i)), mx_ref.quantize(e[:, :4 * NC])) + mx_ref.matmul(mx_ref.quantize(cut(w, 2 * i + 1)), mx_ref.quantize(e[:, 4 * D:4 * D + 4 * NC]))
def setup_inputs(rng):
    def f(*shape):
        return mx_ref.flush((rng.standard_normal(shape, dtype=np.float32) * np.exp2(rng.integers(-2, 3, shape[:-1] + (1,)))).astype(BF))
    return {"x": f(N, 128, 4 * NC), "wa": np.broadcast_to(f(1, 128, 2 * G * 512), (N, 128, 2 * G * 512)).copy(), "wb": f(N, 128, 2 * 512)}
def setup_inputs_blocks(rng):
    d = setup_inputs(rng)
    for k in ("x", "wb"): d[k] = mx_ref.spread(d[k], rng, 2)
    return d
def setup_inputs_wide(rng):
    d = setup_inputs(rng)
    for k in ("wb",): d[k] = mx_ref.flush((d[k].astype(np.float32) * np.exp2(rng.integers(-6, 7, (N, 1, 1))).astype(np.float32)).astype(BF))
    return d
def setup_inputs_zeros(rng):
    d = setup_inputs(rng); v = d["x"].reshape(N, 128, -1, 4).copy()
    v[np.broadcast_to((rng.random((N, 1, v.shape[2], 1)) < 0.33), v.shape)] = 0
    d["x"] = v.reshape(d["x"].shape)
    return d
def reference(x, wa, wb):
    edge = lambda t, r: np.concatenate([t[(r - 1) % N][:, 4 * (NC - D):], t[r]], axis=1)
    u = [tile(act([taps(wa[r], i, edge(x, r)) for i in range(G)])) for r in range(N)]
    y = np.zeros((N, 128, NC), np.float32)
    for r in range(N):
        y[r] = taps(wb[r], 0, edge(u, r))
    return {"y": y}

@@ -1,0 +1,142 @@
+from concourse.mybir import dt, AluOpType, ActivationFunctionType
+
+NC = 256
+D = 4
+H = 2 * D
+L = 16
+A0 = L - H
+C = 0.031
+NL = 128
+
+SCRATCH = {
+    "xs": ("sbuf", [128, 4 * NC], "bfloat16"),
+    "was": ("sbuf", [128, 2048], "bfloat16"),
+    "wbs": ("sbuf", [128, 1024], "bfloat16"),
+    "ub": ("sbuf", [128, 4 * (NC + D)], "bfloat16"),
+    "yo": ("sbuf", [128, NC], "float32"),
+    "qx": ("sbuf", [128, L + NC], "float8_e4m3fn_x4"),
+    "sx": ("sbuf", [128, L + NC], "uint8"),
+    "qa": ("sbuf", [128, 512], "float8_e4m3fn_x4"),
+    "sa": ("sbuf", [128, 512], "uint8"),
+    "qb": ("sbuf", [128, 256], "float8_e4m3fn_x4"),
+    "sb": ("sbuf", [128, 256], "uint8"),
+    "qu": ("sbuf", [128, NC - D], "float8_e4m3fn_x4"),
+    "su": ("sbuf", [128, NC - D], "uint8"),
+    "ql": ("sbuf", [128, NL + D], "float8_e4m3fn_x4"),
+    "sl": ("sbuf", [128, NL + D], "uint8"),
+    "z0": ("psum", [128, 512], "float32"),
+    "z1a": ("psum", [128, 512], "float32"),
+    "z1b": ("psum", [128, 512], "float32"),
+    "zl0": ("psum", [128, 512], "float32"),
+    "zl1": ("psum", [128, 512], "float32"),
+    "ym": ("psum", [128, 512], "float32"),
+    "yl": ("psum", [128, 512], "float32"),
+}
+SEMAPHORES = ["go", "l_xr", "l_xl", "l_a0", "l_a1", "l_b", "q_xr", "q_xl", "q_a0", "q_a1", "q_b", "q_u", "q_l",
+              "m_z0", "m_z1a", "m_z1b", "m_zl0", "m_zl1", "m_ym", "m_yl", "act_s", "act_v", "lact_s", "lact_v",
+              "c_ym", "c_yl", "st_m", "st_l", "arrived", "sent"]
+
+
+def rank_program(g, core, T, topo):
+    rank = T.rank_of(core)
+    if rank is None:
+        return
+    s = T.sem
+    nxt = T.cores[(rank + 1) % len(T.cores)]
+    rid, pid, _ = topo.addr(nxt)
+    mask = topo.mask(core, nxt)
+    relu = ActivationFunctionType.Relu
+
+    def usl(b, lo, hi):
+        return T.ub[:, 4 * lo + b:4 * hi:4]
+
+    def mm(out, w, sw, k, x, sx, a, n, start, stop):
+        return g.tensor.matmul_mx(out, w[:, 128 * k:128 * k + 128], sw[:, 128 * k:128 * k + 128],
+                                  x[:, a:a + n], sx[:, a:a + n], start, stop)
+
+    def taps(out, w, sw, i, x, sx, a, n):
+        mm(out, w, sw, 2 * i, x, sx, a, n, True, False)
+        return mm(out, w, sw, 2 * i + 1, x, sx, a + D, n, False, True)
+
+    M = NC - NL
+    g.sync.dma_start(T.xs[:, 4 * M:4 * NC], T.x[:, 4 * M:4 * NC]).then_inc(s.l_xr, 16)
+    g.sync.sem_inc(s.go, 1)
+    g.sync.dma_start(T.xs[:, 0:4 * M], T.x[:, 0:4 * M]).then_inc(s.l_xl, 16)
+    g.sync.dma_start(T.was[:, 1024:2048], T.wa[:, 1024:2048]).then_inc(s.l_a1, 16)
+
+    g.scalar.wait_ge(s.go, 1)
+    g.scalar.dma_start(T.was[:, 0:1024], T.wa[:, 0:1024]).then_inc(s.l_a0, 16)
+    g.scalar.wait_ge(s.l_xr, 16)
+    g.scalar.dma_start(T.wbs[:], T.wb[:]).then_inc(s.l_b, 16)
+
+    g.wait_ge(s.q_xr, 1)
+    g.remote_dma(T.qx[:, A0:L].bitcast(dt.uint8), T.qx[:, L + NC - H:L + NC].bitcast(dt.uint8),
+                 s.arrived, s.sent, pid, rid, mask)
+    g.remote_dma(T.sx[:, A0:L], T.sx[:, L + NC - H:L + NC], s.arrived, s.sent, pid, rid, mask)
+    n_eng = bin(mask).count("1")
+    g.wait_ge(s.sent, 2 * n_eng)
+
+    v = g.vector
+    v.wait_ge(s.l_xr, 16)
+    v.quantize_mx(T.qx[:, L + M:L + NC], T.sx[:, L + M:L + NC], T.xs[:, 4 * M:4 * NC]).then_inc(s.q_xr, 1)
+    v.wait_ge(s.l_xl, 16)
+    v.quantize_mx(T.qx[:, L:L + M], T.sx[:, L:L + M], T.xs[:, 0:4 * M]).then_inc(s.q_xl, 1)
+    v.wait_ge(s.l_a0, 16)
+    v.quantize_mx(T.qa[:, 0:256], T.sa[:, 0:256], T.was[:, 0:1024]).then_inc(s.q_a0, 1)
+    v.wait_ge(s.l_a1, 16)
+    v.quantize_mx(T.qa[:, 256:512], T.sa[:, 256:512], T.was[:, 1024:2048]).then_inc(s.q_a1, 1)
+
+    t = g.tensor
+    t.wait_ge(s.q_xr, 1)
+    t.wait_ge(s.q_xl, 1)
+    t.wait_ge(s.q_a0, 1)
+    taps(T.z0[:, 0:NC - D], T.qa, T.sa, 0, T.qx, T.sx, L, NC - D).then_inc(s.m_z0, 1)
+    t.wait_ge(s.q_a1, 1)
+    taps(T.z1a[:, 0:NL], T.qa, T.sa, 1, T.qx, T.sx, L, NL).then_inc(s.m_z1a, 1)
+    taps(T.z1b[:, 0:NL], T.qa, T.sa, 1, T.qx, T.sx, L + NC - D - NL, NL).then_inc(s.m_z1b, 1)
+
+    EH = D + NC - NL
+    a = g.scalar
+    a.wait_ge(s.m_z0, 1)
+    a.activation(usl(0, H, NC + D), T.z0[:, 0:NC - D], relu, scale=C).then_inc(s.act_s, 1)
+    a.activation(usl(1, H, NC + D), T.z0[:, 0:NC - D], relu, scale=-C).then_inc(s.act_s, 1)
+    a.wait_ge(s.m_z1a, 1)
+    a.activation(usl(2, H, EH), T.z1a[:, 0:EH - H], relu, scale=C).then_inc(s.act_s, 1)
+    a.activation(usl(3, H, EH), T.z1a[:, 0:EH - H], relu, scale=-C).then_inc(s.act_s, 1)
+    v.wait_ge(s.m_z1b, 1)
+    v.tensor_scalar(usl(2, EH, NC + D), T.z1b[:, 0:NL], C, 0.0, AluOpType.mult, AluOpType.max).then_inc(s.act_v, 1)
+    v.tensor_scalar(usl(3, EH, NC + D), T.z1b[:, 0:NL], -C, 0.0, AluOpType.mult, AluOpType.max).then_inc(s.act_v, 1)
+    v.wait_ge(s.act_v, 2)
+    v.wait_ge(s.act_s, 4)
+    v.quantize_mx(T.qu[:], T.su[:], T.ub[:, 4 * H:4 * (NC + D)]).then_inc(s.q_u, 1)
+    v.wait_ge(s.l_b, 16)
+    v.quantize_mx(T.qb[:], T.sb[:], T.wbs[:]).then_inc(s.q_b, 1)
+
+    t.wait_ge(s.q_u, 1)
+    t.wait_ge(s.q_b, 1)
+    taps(T.ym[:, 0:NC - H], T.qb, T.sb, 0, T.qu, T.su, 0, NC - H).then_inc(s.m_ym, 1)
+    a.wait_ge(s.m_ym, 1)
+    a.activation(T.yo[:, H:NC], T.ym[:, 0:NC - H], ActivationFunctionType.Copy).then_inc(s.c_ym, 1)
+    g.sync.wait_ge(s.c_ym, 1)
+    g.sync.dma_start(T.y[:, H:NC], T.yo[:, H:NC]).then_inc(s.st_m, 16)
+
+    t.wait_ge(s.arrived, 2 * n_eng)
+    taps(T.zl0[:, 0:NL], T.qa, T.sa, 0, T.qx, T.sx, A0, NL).then_inc(s.m_zl0, 1)
+    taps(T.zl1[:, 0:NL], T.qa, T.sa, 1, T.qx, T.sx, A0, NL).then_inc(s.m_zl1, 1)
+    a.wait_ge(s.m_zl0, 1)
+    a.activation(usl(0, 0, H), T.zl0[:, 0:H], relu, scale=C).then_inc(s.lact_s, 1)
+    a.activation(usl(1, 0, H), T.zl0[:, 0:H], relu, scale=-C).then_inc(s.lact_s, 1)
+    v.wait_ge(s.m_zl1, 1)
+    v.tensor_scalar(usl(2, 0, H), T.zl1[:, 0:H], C, 0.0, AluOpType.mult, AluOpType.max).then_inc(s.lact_v, 1)
+    v.tensor_scalar(usl(3, 0, H), T.zl1[:, 0:H], -C, 0.0, AluOpType.mult, AluOpType.max).then_inc(s.lact_v, 1)
+    v.wait_ge(s.lact_s, 2)
+    v.wait_ge(s.lact_v, 2)
+    v.quantize_mx(T.ql[:], T.sl[:], T.ub[:, 0:4 * (NL + D)]).then_inc(s.q_l, 1)
+    t.wait_ge(s.q_l, 1)
+    taps(T.yl[:, 0:NL], T.qb, T.sb, 0, T.ql, T.sl, 0, NL).then_inc(s.m_yl, 1)
+    v.wait_ge(s.m_yl, 1)
+    v.tensor_copy(T.yo[:, 0:H], T.yl[:, 0:H]).then_inc(s.c_yl, 1)
+    a.wait_ge(s.c_yl, 1)
+    a.dma_start(T.y[:, 0:H], T.yo[:, 0:H]).then_inc(s.st_l, 16)
+    a.wait_ge(s.st_l, 16)
+    g.sync.wait_ge(s.st_m, 16)

@@ -6,137 +6,168 @@ H = 2 * D
 L = 16
 A0 = L - H
 C = 0.031
-NL = 128
+W = 128
+M = 128
+NE = NC + D
+NR = NE - M
+TR = M - H
+NXR = NC - TR
+NXL = W + D
 
 SCRATCH = {
-    "xs": ("sbuf", [128, 4 * NC], "bfloat16"),
+    "xr": ("sbuf", [128, 4 * NXR], "bfloat16"),
+    "xl": ("sbuf", [128, 4 * NXL], "bfloat16"),
     "was": ("sbuf", [128, 2048], "bfloat16"),
     "wbs": ("sbuf", [128, 1024], "bfloat16"),
-    "ub": ("sbuf", [128, 4 * (NC + D)], "bfloat16"),
+    "ub": ("sbuf", [128, 4 * NE], "bfloat16"),
     "yo": ("sbuf", [128, NC], "float32"),
-    "qx": ("sbuf", [128, L + NC], "float8_e4m3fn_x4"),
-    "sx": ("sbuf", [128, L + NC], "uint8"),
+    "qxr": ("sbuf", [128, NXR], "float8_e4m3fn_x4"),
+    "sxr": ("sbuf", [128, NXR], "uint8"),
+    "qxl": ("sbuf", [128, L + NXL], "float8_e4m3fn_x4"),
+    "sxl": ("sbuf", [128, L + NXL], "uint8"),
     "qa": ("sbuf", [128, 512], "float8_e4m3fn_x4"),
     "sa": ("sbuf", [128, 512], "uint8"),
     "qb": ("sbuf", [128, 256], "float8_e4m3fn_x4"),
     "sb": ("sbuf", [128, 256], "uint8"),
-    "qu": ("sbuf", [128, NC - D], "float8_e4m3fn_x4"),
-    "su": ("sbuf", [128, NC - D], "uint8"),
-    "ql": ("sbuf", [128, NL + D], "float8_e4m3fn_x4"),
-    "sl": ("sbuf", [128, NL + D], "uint8"),
-    "z0": ("psum", [128, 512], "float32"),
-    "z1a": ("psum", [128, 512], "float32"),
-    "z1b": ("psum", [128, 512], "float32"),
-    "zl0": ("psum", [128, 512], "float32"),
-    "zl1": ("psum", [128, 512], "float32"),
-    "ym": ("psum", [128, 512], "float32"),
-    "yl": ("psum", [128, 512], "float32"),
+    "qr": ("sbuf", [128, NR], "float8_e4m3fn_x4"),
+    "sr": ("sbuf", [128, NR], "uint8"),
+    "ql": ("sbuf", [128, W + D], "float8_e4m3fn_x4"),
+    "sl": ("sbuf", [128, W + D], "uint8"),
+    "qe": ("sbuf", [128, W + D], "float8_e4m3fn_x4"),
+    "se": ("sbuf", [128, W + D], "uint8"),
+    "z0r": ("psum", [128, 512], "float32"),
+    "z1r": ("psum", [128, 512], "float32"),
+    "z0l": ("psum", [128, 512], "float32"),
+    "z1l": ("psum", [128, 512], "float32"),
+    "z0e": ("psum", [128, 512], "float32"),
+    "z1e": ("psum", [128, 512], "float32"),
+    "yr": ("psum", [128, 512], "float32"),
+    "ye": ("psum", [128, 512], "float32"),
 }
-SEMAPHORES = ["go", "l_xr", "l_xl", "l_a0", "l_a1", "l_b", "q_xr", "q_xl", "q_a0", "q_a1", "q_b", "q_u", "q_l",
-              "m_z0", "m_z1a", "m_z1b", "m_zl0", "m_zl1", "m_ym", "m_yl", "act_s", "act_v", "lact_s", "lact_v",
-              "c_ym", "c_yl", "st_m", "st_l", "arrived", "sent"]
+SEMAPHORES = ["l_xr", "l_xl", "l_a0", "l_a1", "l_b", "q_xr", "q_xl", "q_a0", "q_a2", "q_a3", "q_b", "q_ur", "q_ul", "q_ue",
+              "m_z0r", "m_z1r", "m_z0l", "m_z1l", "m_z0e", "m_z1e", "m_yr", "m_yl", "m_ye",
+              "a_0r", "a_1r", "a_l", "a_0e", "a_1e", "c_yr", "c_yl", "c_ye", "st_r", "st_l", "st_e", "arrived", "sent"]
 
 
 def rank_program(g, core, T, topo):
     rank = T.rank_of(core)
     if rank is None:
         return
-    s = T.sem
+    s, v, t, a = T.sem, g.vector, g.tensor, g.scalar
     nxt = T.cores[(rank + 1) % len(T.cores)]
     rid, pid, _ = topo.addr(nxt)
     mask = topo.mask(core, nxt)
-    relu = ActivationFunctionType.Relu
+    n_eng = bin(mask).count("1")
+    relu, copy = ActivationFunctionType.Relu, ActivationFunctionType.Copy
 
     def usl(b, lo, hi):
         return T.ub[:, 4 * lo + b:4 * hi:4]
 
-    def mm(out, w, sw, k, x, sx, a, n, start, stop):
-        return g.tensor.matmul_mx(out, w[:, 128 * k:128 * k + 128], sw[:, 128 * k:128 * k + 128],
-                                  x[:, a:a + n], sx[:, a:a + n], start, stop)
+    def mm(out, w, sw, k, x, sx, c, n, first):
+        return t.matmul_mx(out[:, 0:n], w[:, 128 * k:128 * k + 128], sw[:, 128 * k:128 * k + 128],
+                           x[:, c:c + n], sx[:, c:c + n], first, not first)
 
-    def taps(out, w, sw, i, x, sx, a, n):
-        mm(out, w, sw, 2 * i, x, sx, a, n, True, False)
-        return mm(out, w, sw, 2 * i + 1, x, sx, a + D, n, False, True)
+    def layer1(out, i, x, sx, c, n):
+        mm(out, T.qa, T.sa, 2 * i, x, sx, c, n, True)
+        return mm(out, T.qa, T.sa, 2 * i + 1, x, sx, c + D, n, False)
 
-    M = NC - NL
-    g.sync.dma_start(T.xs[:, 4 * M:4 * NC], T.x[:, 4 * M:4 * NC]).then_inc(s.l_xr, 16)
-    g.sync.sem_inc(s.go, 1)
-    g.sync.dma_start(T.xs[:, 0:4 * M], T.x[:, 0:4 * M]).then_inc(s.l_xl, 16)
+    def layer2(out, x, sx):
+        mm(out, T.qb, T.sb, 0, x, sx, 0, W, True)
+        return mm(out, T.qb, T.sb, 1, x, sx, D, W, False)
+
+    def quant_w(q, sc, w, k, n):
+        return v.quantize_mx(q[:, 128 * k:128 * (k + n)], sc[:, 128 * k:128 * (k + n)], w[:, 512 * k:512 * (k + n)])
+
+    def quant_u(q, sc, lo):
+        return v.quantize_mx(q[:], sc[:], T.ub[:, 4 * lo:4 * (lo + W + D)])
+
+    def steps_s(i, z, lo, hi, sem):
+        a.activation(usl(2 * i, lo, hi), z[:, 0:hi - lo], relu, scale=C).then_inc(sem, 1)
+        a.activation(usl(2 * i + 1, lo, hi), z[:, 0:hi - lo], relu, scale=-C).then_inc(sem, 1)
+
+    def steps_v(i, z, lo, hi, sem):
+        for b, c in ((2 * i, C), (2 * i + 1, -C)):
+            v.tensor_scalar(usl(b, lo, hi), z[:, 0:hi - lo], c, 0.0, AluOpType.mult, AluOpType.max).then_inc(sem, 1)
+
+    g.sync.dma_start(T.xr[:], T.x[:, 4 * TR:4 * NC]).then_inc(s.l_xr, 16)
+    g.sync.dma_start(T.was[:, 0:1024], T.wa[:, 0:1024]).then_inc(s.l_a0, 16)
     g.sync.dma_start(T.was[:, 1024:2048], T.wa[:, 1024:2048]).then_inc(s.l_a1, 16)
-
-    g.scalar.wait_ge(s.go, 1)
-    g.scalar.dma_start(T.was[:, 0:1024], T.wa[:, 0:1024]).then_inc(s.l_a0, 16)
-    g.scalar.wait_ge(s.l_xr, 16)
-    g.scalar.dma_start(T.wbs[:], T.wb[:]).then_inc(s.l_b, 16)
+    g.sync.dma_start(T.xl[:], T.x[:, 0:4 * NXL]).then_inc(s.l_xl, 16)
+    a.wait_ge(s.l_xr, 16)
+    a.dma_start(T.wbs[:], T.wb[:]).then_inc(s.l_b, 16)
 
     g.wait_ge(s.q_xr, 1)
-    g.remote_dma(T.qx[:, A0:L].bitcast(dt.uint8), T.qx[:, L + NC - H:L + NC].bitcast(dt.uint8),
+    g.remote_dma(T.qxl[:, A0:L].bitcast(dt.uint8), T.qxr[:, NXR - H:NXR].bitcast(dt.uint8),
                  s.arrived, s.sent, pid, rid, mask)
-    g.remote_dma(T.sx[:, A0:L], T.sx[:, L + NC - H:L + NC], s.arrived, s.sent, pid, rid, mask)
-    n_eng = bin(mask).count("1")
+    g.remote_dma(T.sxl[:, A0:L], T.sxr[:, NXR - H:NXR], s.arrived, s.sent, pid, rid, mask)
     g.wait_ge(s.sent, 2 * n_eng)
 
-    v = g.vector
     v.wait_ge(s.l_xr, 16)
-    v.quantize_mx(T.qx[:, L + M:L + NC], T.sx[:, L + M:L + NC], T.xs[:, 4 * M:4 * NC]).then_inc(s.q_xr, 1)
-    v.wait_ge(s.l_xl, 16)
-    v.quantize_mx(T.qx[:, L:L + M], T.sx[:, L:L + M], T.xs[:, 0:4 * M]).then_inc(s.q_xl, 1)
+    v.quantize_mx(T.qxr[:], T.sxr[:], T.xr[:]).then_inc(s.q_xr, 1)
     v.wait_ge(s.l_a0, 16)
-    v.quantize_mx(T.qa[:, 0:256], T.sa[:, 0:256], T.was[:, 0:1024]).then_inc(s.q_a0, 1)
+    quant_w(T.qa, T.sa, T.was, 0, 2).then_inc(s.q_a0, 1)
     v.wait_ge(s.l_a1, 16)
-    v.quantize_mx(T.qa[:, 256:512], T.sa[:, 256:512], T.was[:, 1024:2048]).then_inc(s.q_a1, 1)
-
-    t = g.tensor
-    t.wait_ge(s.q_xr, 1)
-    t.wait_ge(s.q_xl, 1)
-    t.wait_ge(s.q_a0, 1)
-    taps(T.z0[:, 0:NC - D], T.qa, T.sa, 0, T.qx, T.sx, L, NC - D).then_inc(s.m_z0, 1)
-    t.wait_ge(s.q_a1, 1)
-    taps(T.z1a[:, 0:NL], T.qa, T.sa, 1, T.qx, T.sx, L, NL).then_inc(s.m_z1a, 1)
-    taps(T.z1b[:, 0:NL], T.qa, T.sa, 1, T.qx, T.sx, L + NC - D - NL, NL).then_inc(s.m_z1b, 1)
-
-    EH = D + NC - NL
-    a = g.scalar
-    a.wait_ge(s.m_z0, 1)
-    a.activation(usl(0, H, NC + D), T.z0[:, 0:NC - D], relu, scale=C).then_inc(s.act_s, 1)
-    a.activation(usl(1, H, NC + D), T.z0[:, 0:NC - D], relu, scale=-C).then_inc(s.act_s, 1)
-    a.wait_ge(s.m_z1a, 1)
-    a.activation(usl(2, H, EH), T.z1a[:, 0:EH - H], relu, scale=C).then_inc(s.act_s, 1)
-    a.activation(usl(3, H, EH), T.z1a[:, 0:EH - H], relu, scale=-C).then_inc(s.act_s, 1)
-    v.wait_ge(s.m_z1b, 1)
-    v.tensor_scalar(usl(2, EH, NC + D), T.z1b[:, 0:NL], C, 0.0, AluOpType.mult, AluOpType.max).then_inc(s.act_v, 1)
-    v.tensor_scalar(usl(3, EH, NC + D), T.z1b[:, 0:NL], -C, 0.0, AluOpType.mult, AluOpType.max).then_inc(s.act_v, 1)
-    v.wait_ge(s.act_v, 2)
-    v.wait_ge(s.act_s, 4)
-    v.quantize_mx(T.qu[:], T.su[:], T.ub[:, 4 * H:4 * (NC + D)]).then_inc(s.q_u, 1)
+    quant_w(T.qa, T.sa, T.was, 2, 1).then_inc(s.q_a2, 1)
+    quant_w(T.qa, T.sa, T.was, 3, 1).then_inc(s.q_a3, 1)
+    v.wait_ge(s.l_xl, 16)
+    v.quantize_mx(T.qxl[:, L:L + NXL], T.sxl[:, L:L + NXL], T.xl[:]).then_inc(s.q_xl, 1)
+    v.wait_ge(s.m_z1r, 1)
+    steps_v(1, T.z1r, M, NE, s.a_1r)
+    v.wait_ge(s.a_0r, 2)
+    v.wait_ge(s.a_1r, 2)
+    quant_u(T.qr, T.sr, M).then_inc(s.q_ur, 1)
     v.wait_ge(s.l_b, 16)
-    v.quantize_mx(T.qb[:], T.sb[:], T.wbs[:]).then_inc(s.q_b, 1)
+    quant_w(T.qb, T.sb, T.wbs, 0, 2).then_inc(s.q_b, 1)
+    v.wait_ge(s.a_l, 4)
+    quant_u(T.ql, T.sl, H).then_inc(s.q_ul, 1)
+    v.wait_ge(s.m_z1e, 1)
+    steps_v(1, T.z1e, 0, H, s.a_1e)
+    v.wait_ge(s.a_0e, 2)
+    v.wait_ge(s.a_1e, 2)
+    quant_u(T.qe, T.se, 0).then_inc(s.q_ue, 1)
+    v.wait_ge(s.m_ye, 1)
+    v.tensor_copy(T.yo[:, 0:H], T.ye[:, 0:H]).then_inc(s.c_ye, 1)
 
-    t.wait_ge(s.q_u, 1)
+    t.wait_ge(s.q_xr, 1)
+    t.wait_ge(s.q_a0, 1)
+    layer1(T.z0r, 0, T.qxr, T.sxr, 0, NR).then_inc(s.m_z0r, 1)
+    t.wait_ge(s.q_a2, 1)
+    mm(T.z1r, T.qa, T.sa, 2, T.qxr, T.sxr, 0, NR, True)
+    t.wait_ge(s.q_a3, 1)
+    mm(T.z1r, T.qa, T.sa, 3, T.qxr, T.sxr, D, NR, False).then_inc(s.m_z1r, 1)
+    t.wait_ge(s.q_xl, 1)
+    layer1(T.z0l, 0, T.qxl, T.sxl, L, W).then_inc(s.m_z0l, 1)
+    layer1(T.z1l, 1, T.qxl, T.sxl, L, W).then_inc(s.m_z1l, 1)
+    t.wait_ge(s.q_ur, 1)
     t.wait_ge(s.q_b, 1)
-    taps(T.ym[:, 0:NC - H], T.qb, T.sb, 0, T.qu, T.su, 0, NC - H).then_inc(s.m_ym, 1)
-    a.wait_ge(s.m_ym, 1)
-    a.activation(T.yo[:, H:NC], T.ym[:, 0:NC - H], ActivationFunctionType.Copy).then_inc(s.c_ym, 1)
-    g.sync.wait_ge(s.c_ym, 1)
-    g.sync.dma_start(T.y[:, H:NC], T.yo[:, H:NC]).then_inc(s.st_m, 16)
-
+    layer2(T.yr, T.qr, T.sr).then_inc(s.m_yr, 1)
     t.wait_ge(s.arrived, 2 * n_eng)
-    taps(T.zl0[:, 0:NL], T.qa, T.sa, 0, T.qx, T.sx, A0, NL).then_inc(s.m_zl0, 1)
-    taps(T.zl1[:, 0:NL], T.qa, T.sa, 1, T.qx, T.sx, A0, NL).then_inc(s.m_zl1, 1)
-    a.wait_ge(s.m_zl0, 1)
-    a.activation(usl(0, 0, H), T.zl0[:, 0:H], relu, scale=C).then_inc(s.lact_s, 1)
-    a.activation(usl(1, 0, H), T.zl0[:, 0:H], relu, scale=-C).then_inc(s.lact_s, 1)
-    v.wait_ge(s.m_zl1, 1)
-    v.tensor_scalar(usl(2, 0, H), T.zl1[:, 0:H], C, 0.0, AluOpType.mult, AluOpType.max).then_inc(s.lact_v, 1)
-    v.tensor_scalar(usl(3, 0, H), T.zl1[:, 0:H], -C, 0.0, AluOpType.mult, AluOpType.max).then_inc(s.lact_v, 1)
-    v.wait_ge(s.lact_s, 2)
-    v.wait_ge(s.lact_v, 2)
-    v.quantize_mx(T.ql[:], T.sl[:], T.ub[:, 0:4 * (NL + D)]).then_inc(s.q_l, 1)
-    t.wait_ge(s.q_l, 1)
-    taps(T.yl[:, 0:NL], T.qb, T.sb, 0, T.ql, T.sl, 0, NL).then_inc(s.m_yl, 1)
-    v.wait_ge(s.m_yl, 1)
-    v.tensor_copy(T.yo[:, 0:H], T.yl[:, 0:H]).then_inc(s.c_yl, 1)
-    a.wait_ge(s.c_yl, 1)
-    a.dma_start(T.y[:, 0:H], T.yo[:, 0:H]).then_inc(s.st_l, 16)
-    a.wait_ge(s.st_l, 16)
-    g.sync.wait_ge(s.st_m, 16)
+    layer1(T.z0e, 0, T.qxl, T.sxl, A0, W).then_inc(s.m_z0e, 1)
+    layer1(T.z1e, 1, T.qxl, T.sxl, A0, W).then_inc(s.m_z1e, 1)
+    t.wait_ge(s.q_ul, 1)
+    layer2(T.z0r, T.ql, T.sl).then_inc(s.m_yl, 1)
+    t.wait_ge(s.q_ue, 1)
+    layer2(T.ye, T.qe, T.se).then_inc(s.m_ye, 1)
+
+    a.wait_ge(s.m_z0r, 1)
+    steps_s(0, T.z0r, M, NE, s.a_0r)
+    a.wait_ge(s.m_z0l, 1)
+    steps_s(0, T.z0l, H, M, s.a_l)
+    a.wait_ge(s.m_z1l, 1)
+    steps_s(1, T.z1l, H, M, s.a_l)
+    a.wait_ge(s.m_yr, 1)
+    a.activation(T.yo[:, M:NC], T.yr[:, 0:W], copy).then_inc(s.c_yr, 1)
+    a.wait_ge(s.m_z0e, 1)
+    steps_s(0, T.z0e, 0, H, s.a_0e)
+    a.wait_ge(s.m_yl, 1)
+    a.activation(T.yo[:, H:M], T.z0r[:, 0:M - H], copy).then_inc(s.c_yl, 1)
+    a.wait_ge(s.c_ye, 1)
+    a.dma_start(T.y[:, 0:H], T.yo[:, 0:H]).then_inc(s.st_e, 16)
+    a.wait_ge(s.st_e, 16)
+
+    g.sync.wait_ge(s.c_yr, 1)
+    g.sync.dma_start(T.y[:, M:NC], T.yo[:, M:NC]).then_inc(s.st_r, 16)
+    g.sync.wait_ge(s.c_yl, 1)
+    g.sync.dma_start(T.y[:, H:M], T.yo[:, H:M]).then_inc(s.st_l, 16)
+    g.sync.wait_ge(s.st_r, 16)
+    g.sync.wait_ge(s.st_l, 16)

from concourse.mybir import dt, AluOpType, ActivationFunctionType

NC = 256
D = 4
H = 2 * D
L = 16
A0 = L - H
C = 0.031
W = 128
M = 128
NE = NC + D
NR = NE - M
TR = M - H
NXR = NC - TR
NXL = W + D

SCRATCH = {
    "xr": ("sbuf", [128, 4 * NXR], "bfloat16"),
    "xl": ("sbuf", [128, 4 * NXL], "bfloat16"),
    "was": ("sbuf", [128, 2048], "bfloat16"),
    "wbs": ("sbuf", [128, 1024], "bfloat16"),
    "ub": ("sbuf", [128, 4 * NE], "bfloat16"),
    "yo": ("sbuf", [128, NC], "float32"),
    "qxr": ("sbuf", [128, NXR], "float8_e4m3fn_x4"),
    "sxr": ("sbuf", [128, NXR], "uint8"),
    "qxl": ("sbuf", [128, L + NXL], "float8_e4m3fn_x4"),
    "sxl": ("sbuf", [128, L + NXL], "uint8"),
    "qa": ("sbuf", [128, 512], "float8_e4m3fn_x4"),
    "sa": ("sbuf", [128, 512], "uint8"),
    "qb": ("sbuf", [128, 256], "float8_e4m3fn_x4"),
    "sb": ("sbuf", [128, 256], "uint8"),
    "qr": ("sbuf", [128, NR], "float8_e4m3fn_x4"),
    "sr": ("sbuf", [128, NR], "uint8"),
    "ql": ("sbuf", [128, W + D], "float8_e4m3fn_x4"),
    "sl": ("sbuf", [128, W + D], "uint8"),
    "qe": ("sbuf", [128, W + D], "float8_e4m3fn_x4"),
    "se": ("sbuf", [128, W + D], "uint8"),
    "z0r": ("psum", [128, 512], "float32"),
    "z1r": ("psum", [128, 512], "float32"),
    "z0l": ("psum", [128, 512], "float32"),
    "z1l": ("psum", [128, 512], "float32"),
    "z0e": ("psum", [128, 512], "float32"),
    "z1e": ("psum", [128, 512], "float32"),
    "yr": ("psum", [128, 512], "float32"),
    "ye": ("psum", [128, 512], "float32"),
}
SEMAPHORES = ["l_xr", "l_xl", "l_a0", "l_a1", "l_b", "q_xr", "q_xl", "q_a0", "q_a2", "q_a3", "q_b", "q_ur", "q_ul", "q_ue",
              "m_z0r", "m_z1r", "m_z0l", "m_z1l", "m_z0e", "m_z1e", "m_yr", "m_yl", "m_ye",
              "a_0r", "a_1r", "a_l", "a_0e", "a_1e", "c_yr", "c_yl", "c_ye", "st_r", "st_l", "st_e", "arrived", "sent"]


def rank_program(g, core, T, topo):
    rank = T.rank_of(core)
    if rank is None:
        return
    s, v, t, a = T.sem, g.vector, g.tensor, g.scalar
    nxt = T.cores[(rank + 1) % len(T.cores)]
    rid, pid, _ = topo.addr(nxt)
    mask = topo.mask(core, nxt)
    n_eng = bin(mask).count("1")
    relu, copy = ActivationFunctionType.Relu, ActivationFunctionType.Copy

    def usl(b, lo, hi):
        return T.ub[:, 4 * lo + b:4 * hi:4]

    def mm(out, w, sw, k, x, sx, c, n, first):
        return t.matmul_mx(out[:, 0:n], w[:, 128 * k:128 * k + 128], sw[:, 128 * k:128 * k + 128],
                           x[:, c:c + n], sx[:, c:c + n], first, not first)

    def layer1(out, i, x, sx, c, n):
        mm(out, T.qa, T.sa, 2 * i, x, sx, c, n, True)
        return mm(out, T.qa, T.sa, 2 * i + 1, x, sx, c + D, n, False)

    def layer2(out, x, sx):
        mm(out, T.qb, T.sb, 0, x, sx, 0, W, True)
        return mm(out, T.qb, T.sb, 1, x, sx, D, W, False)

    def quant_w(q, sc, w, k, n):
        return v.quantize_mx(q[:, 128 * k:128 * (k + n)], sc[:, 128 * k:128 * (k + n)], w[:, 512 * k:512 * (k + n)])

    def quant_u(q, sc, lo):
        return v.quantize_mx(q[:], sc[:], T.ub[:, 4 * lo:4 * (lo + W + D)])

    def steps_s(i, z, lo, hi, sem):
        a.activation(usl(2 * i, lo, hi), z[:, 0:hi - lo], relu, scale=C).then_inc(sem, 1)
        a.activation(usl(2 * i + 1, lo, hi), z[:, 0:hi - lo], relu, scale=-C).then_inc(sem, 1)

    def steps_v(i, z, lo, hi, sem):
        for b, c in ((2 * i, C), (2 * i + 1, -C)):
            v.tensor_scalar(usl(b, lo, hi), z[:, 0:hi - lo], c, 0.0, AluOpType.mult, AluOpType.max).then_inc(sem, 1)

    g.sync.dma_start(T.xr[:], T.x[:, 4 * TR:4 * NC]).then_inc(s.l_xr, 16)
    g.sync.dma_start(T.was[:, 0:1024], T.wa[:, 0:1024]).then_inc(s.l_a0, 16)
    g.sync.dma_start(T.was[:, 1024:2048], T.wa[:, 1024:2048]).then_inc(s.l_a1, 16)
    g.sync.dma_start(T.xl[:], T.x[:, 0:4 * NXL]).then_inc(s.l_xl, 16)
    a.wait_ge(s.l_xr, 16)
    a.dma_start(T.wbs[:], T.wb[:]).then_inc(s.l_b, 16)

    g.wait_ge(s.q_xr, 1)
    g.remote_dma(T.qxl[:, A0:L].bitcast(dt.uint8), T.qxr[:, NXR - H:NXR].bitcast(dt.uint8),
                 s.arrived, s.sent, pid, rid, mask)
    g.remote_dma(T.sxl[:, A0:L], T.sxr[:, NXR - H:NXR], s.arrived, s.sent, pid, rid, mask)
    g.wait_ge(s.sent, 2 * n_eng)

    v.wait_ge(s.l_xr, 16)
    v.quantize_mx(T.qxr[:], T.sxr[:], T.xr[:]).then_inc(s.q_xr, 1)
    v.wait_ge(s.l_a0, 16)
    quant_w(T.qa, T.sa, T.was, 0, 2).then_inc(s.q_a0, 1)
    v.wait_ge(s.l_a1, 16)
    quant_w(T.qa, T.sa, T.was, 2, 1).then_inc(s.q_a2, 1)
    quant_w(T.qa, T.sa, T.was, 3, 1).then_inc(s.q_a3, 1)
    v.wait_ge(s.l_xl, 16)
    v.quantize_mx(T.qxl[:, L:L + NXL], T.sxl[:, L:L + NXL], T.xl[:]).then_inc(s.q_xl, 1)
    v.wait_ge(s.m_z1r, 1)
    steps_v(1, T.z1r, M, NE, s.a_1r)
    v.wait_ge(s.a_0r, 2)
    v.wait_ge(s.a_1r, 2)
    quant_u(T.qr, T.sr, M).then_inc(s.q_ur, 1)
    v.wait_ge(s.l_b, 16)
    quant_w(T.qb, T.sb, T.wbs, 0, 2).then_inc(s.q_b, 1)
    v.wait_ge(s.a_l, 4)
    quant_u(T.ql, T.sl, H).then_inc(s.q_ul, 1)
    v.wait_ge(s.m_z1e, 1)
    steps_v(1, T.z1e, 0, H, s.a_1e)
    v.wait_ge(s.a_0e, 2)
    v.wait_ge(s.a_1e, 2)
    quant_u(T.qe, T.se, 0).then_inc(s.q_ue, 1)
    v.wait_ge(s.m_ye, 1)
    v.tensor_copy(T.yo[:, 0:H], T.ye[:, 0:H]).then_inc(s.c_ye, 1)

    t.wait_ge(s.q_xr, 1)
    t.wait_ge(s.q_a0, 1)
    layer1(T.z0r, 0, T.qxr, T.sxr, 0, NR).then_inc(s.m_z0r, 1)
    t.wait_ge(s.q_a2, 1)
    mm(T.z1r, T.qa, T.sa, 2, T.qxr, T.sxr, 0, NR, True)
    t.wait_ge(s.q_a3, 1)
    mm(T.z1r, T.qa, T.sa, 3, T.qxr, T.sxr, D, NR, False).then_inc(s.m_z1r, 1)
    t.wait_ge(s.q_xl, 1)
    layer1(T.z0l, 0, T.qxl, T.sxl, L, W).then_inc(s.m_z0l, 1)
    layer1(T.z1l, 1, T.qxl, T.sxl, L, W).then_inc(s.m_z1l, 1)
    t.wait_ge(s.q_ur, 1)
    t.wait_ge(s.q_b, 1)
    layer2(T.yr, T.qr, T.sr).then_inc(s.m_yr, 1)
    t.wait_ge(s.arrived, 2 * n_eng)
    layer1(T.z0e, 0, T.qxl, T.sxl, A0, W).then_inc(s.m_z0e, 1)
    layer1(T.z1e, 1, T.qxl, T.sxl, A0, W).then_inc(s.m_z1e, 1)
    t.wait_ge(s.q_ul, 1)
    layer2(T.z0r, T.ql, T.sl).then_inc(s.m_yl, 1)
    t.wait_ge(s.q_ue, 1)
    layer2(T.ye, T.qe, T.se).then_inc(s.m_ye, 1)

    a.wait_ge(s.m_z0r, 1)
    steps_s(0, T.z0r, M, NE, s.a_0r)
    a.wait_ge(s.m_z0l, 1)
    steps_s(0, T.z0l, H, M, s.a_l)
    a.wait_ge(s.m_z1l, 1)
    steps_s(1, T.z1l, H, M, s.a_l)
    a.wait_ge(s.m_yr, 1)
    a.activation(T.yo[:, M:NC], T.yr[:, 0:W], copy).then_inc(s.c_yr, 1)
    a.wait_ge(s.m_z0e, 1)
    steps_s(0, T.z0e, 0, H, s.a_0e)
    a.wait_ge(s.m_yl, 1)
    a.activation(T.yo[:, H:M], T.z0r[:, 0:M - H], copy).then_inc(s.c_yl, 1)
    a.wait_ge(s.c_ye, 1)
    a.dma_start(T.y[:, 0:H], T.yo[:, 0:H]).then_inc(s.st_e, 16)
    a.wait_ge(s.st_e, 16)

    g.sync.wait_ge(s.c_yr, 1)
    g.sync.dma_start(T.y[:, M:NC], T.yo[:, M:NC]).then_inc(s.st_r, 16)
    g.sync.wait_ge(s.c_yl, 1)
    g.sync.dma_start(T.y[:, H:M], T.yo[:, H:M]).then_inc(s.st_l, 16)
    g.sync.wait_ge(s.st_r, 16)
    g.sync.wait_ge(s.st_l, 16)
